import numpy as np
import ml_dtypes


def mxq(x, axis, fmt="e4m3"):
    dtype, down = {"e4m3": (ml_dtypes.float8_e4m3fn, 7), "e5m2": (ml_dtypes.float8_e5m2, 14)}[fmt]
    v = np.moveaxis(np.asarray(x, np.float32).astype(ml_dtypes.bfloat16).astype(np.float64), axis, -1)
    blocks = v.reshape(v.shape[:-1] + (-1, 32))
    amax = np.abs(blocks).max(-1, keepdims=True)
    byte = np.maximum(np.where(amax > 0, np.frexp(amax)[1] - 1 + 127, 0) - down, 1)
    scale = np.exp2(byte - 127.0)
    codes = (blocks / scale).astype(np.float32).astype(dtype).astype(np.float64)
    return np.moveaxis((codes * scale).reshape(v.shape), -1, axis)


WIDE = False


def mx_kscale(k):
    if not WIDE:
        return np.ones(k)
    levels = np.array([10, -10, 5, -5, 0])
    if k % 512:
        return np.exp2(np.random.permutation(np.resize(levels, k // 32))).repeat(32)
    a = np.empty((k // 512, 16))
    for p in range(k // 512):
        a[p, :8] = np.random.permutation(np.resize(levels, 8))
        for g in range(8):
            far = levels[np.abs(levels - a[p, g]) >= 10]
            a[p, g + 8] = far[np.random.randint(len(far))]
    return np.exp2(a.ravel()).repeat(32)


def f64(x):
    return np.asarray(x).astype(np.float64)


def striped(idx):
    return np.tile(idx.reshape(-1, 16).T, (8, 1)).astype(np.uint16)


def unstriped(offs):
    return offs[:16].T.reshape(-1).astype(np.int64)


E2M1 = np.array([0.0, 0.5, 1.0, 1.5, 2.0, 3.0, 4.0, 6.0, -0.0, -0.5, -1.0, -1.5, -2.0, -3.0, -4.0, -6.0])


def pack_weight(w, fmt):
    k, n = w.shape
    w = f64(np.asarray(w, np.float32).astype(ml_dtypes.bfloat16)).reshape(k // 32, 32, n)
    amax = np.abs(w).max(1)
    if fmt == "e4m3":
        byte = np.frexp(amax)[1] - 1 + 127 - 7
    else:
        mant, ex = np.frexp(amax / 6.0)
        byte = np.where(mant > 0.5, ex, ex - 1) + 127
    byte = np.clip(np.where(amax > 0, byte, 1), 1, 254)
    scaled = (w * np.exp2(127.0 - byte)[:, None, :]).reshape(k, n).astype(np.float32)
    by_word = np.ascontiguousarray(scaled.reshape(k // 512, 128, 4, n).transpose(0, 1, 3, 2))
    if fmt == "e4m3":
        words = by_word.astype(ml_dtypes.float8_e4m3fn).view(np.uint8)
    else:
        c = by_word.astype(ml_dtypes.float4_e2m1fn).view(np.uint8) & 0xF
        words = (c[..., 0::2] | (c[..., 1::2] << 4)).reshape(k // 512, 128, 2 * n)
    return np.ascontiguousarray(words), np.ascontiguousarray(byte.astype(np.uint8).reshape(k // 512, 16, n))


def unpack_weight(words, scales, fmt):
    g, _, n = scales.shape
    words = np.ascontiguousarray(words).reshape(g, 128, n, -1)
    if fmt == "e4m3":
        vals = words.view(ml_dtypes.float8_e4m3fn).astype(np.float64)
    else:
        nib = np.empty((g, 128, n, 4), np.uint8)
        nib[..., 0::2] = words & 0xF
        nib[..., 1::2] = words >> 4
        vals = E2M1[nib]
    vals = vals * np.repeat(np.exp2(scales.astype(np.float64) - 127.0), 8, axis=1)[..., None]
    return vals.transpose(0, 1, 3, 2).reshape(g * 512, n)


def gelu(v):
    return 0.5 * v * (1.0 + np.tanh(np.sqrt(2.0 / np.pi) * (v + 0.044715 * v**3)))


def twice(P):
    return np.random.permutation(np.repeat(np.arange(P), 2))


K, H, T, S, P = 1536, 512, 4096, 1024, 512


def setup_inputs():
    n = np.random.standard_normal
    s = mx_kscale(K)[:, None]
    u = mx_kscale(H)[:, None]
    d = {}
    d["tab_words"], d["tab_scales"] = pack_weight(n((K, T)) * s, "e4m3")
    d["offs"] = striped(np.random.permutation(T)[:S])
    perm = np.random.permutation(S)
    d["pos1"] = striped(perm[:P])
    d["pos2"] = striped(perm[P:2 * P])
    d["pos3"] = striped(twice(P))
    d["wa_words"], d["wa_scales"] = pack_weight(0.6 * n((K, H)) / K**0.5 / s, "e2m1")
    d["wb"] = (0.56 * n((K, H)) / K**0.5 / s).astype(np.float32)
    d["gain"] = (u[:, 0] * np.exp(0.3 * n(H))).astype(np.float32)
    d["w2"] = (0.9 * n((H, H)) / H**0.5 / u).astype(np.float32)
    return d


def reference(tab_words, tab_scales, offs, pos1, pos2, pos3, wa_words, wa_scales, wb, gain, w2):
    v = unpack_weight(tab_words, tab_scales, "e4m3")[:, unstriped(offs)]
    wa = unpack_weight(wa_words, wa_scales, "e2m1")
    qb = mxq(f64(wb), 0, "e4m3")
    level = wa.T @ v
    phase = qb.T @ v
    hs = level + np.sin(phase)
    h = f64(gain)[:, None] * hs
    diff = np.abs(h[:, unstriped(pos1)] - h[:, unstriped(pos2)])
    y = mxq(f64(w2), 0, "e4m3").T @ mxq(diff, 0, "e4m3")
    return np.square(hs) - y[:, unstriped(pos3)]

@@ -1,0 +1,339 @@
+import math
+from contextlib import ExitStack
+
+import concourse.mybir as mybir
+
+K, H, T, S, LAYS = 1536, 512, 4096, 1024, 512
+FLOPS = 2 * (2 * K * H * S + H * H * LAYS)
+
+F32 = mybir.dt.float32
+BF16 = mybir.dt.bfloat16
+I32 = mybir.dt.int32
+U32 = mybir.dt.uint32
+U16 = mybir.dt.uint16
+U8 = mybir.dt.uint8
+FP8X4 = mybir.dt.float8_e4m3fn_x4
+FP4X4 = mybir.dt.float4_e2m1fn_x4
+ACT = mybir.ActivationFunctionType
+ALU = mybir.AluOpType
+
+P = 128
+PACK = 4
+PASSES = K // (P * PACK)
+BANK = 512
+HALVES = S // BANK
+SPARE = 16
+W2_PARTS = ((0, 128), (128, 128), (256, 256))
+LAY_CHUNKS = ((0, 256), (256, 128), (384, 128))
+
+
+def tile_list_rope_lay_anomaly_kernel(
+    tc, tab_words, tab_scales, offs, pos1, pos2, pos3, wa_words, wa_scales, wb, gain, w2, out
+):
+    nc = tc.nc
+    with ExitStack() as ctx:
+        keep = ctx.enter_context(tc.tile_pool(name="keep", bufs=1))
+        ring = ctx.enter_context(tc.tile_pool(name="ring", bufs=4))
+        psum = ctx.enter_context(tc.psum_pool(name="psum", bufs=4))
+
+        def held(name, shape, dtype):
+            return keep.tile(shape, dtype, name=name, align_bytes=64)
+
+        idx = keep.tile([P, S // 16], U16, name="idx")
+        p1 = keep.tile([P, LAYS // 16], U16, name="p1")
+        p2 = keep.tile([P, LAYS // 16], U16, name="p2")
+        p3 = keep.tile([P, S // 16], U16, name="p3")
+        gain_sb = held("gain_sb", [P, PACK], F32)
+        tab = [held("tab%d" % a, [P, T], I32) for a in range(PASSES)]
+        tab_sc = held("tab_sc", [P, T], U8)
+        wa_raw = held("wa_raw", [P, PASSES, 2 * H], U8)
+        wa_sc_raw = held("wa_sc_raw", [P, PASSES, H], U8)
+        wb_raw = [held("wb_raw%d" % a, [P, PACK, H], F32) for a in range(PASSES - 1)]
+        wb_last = [held("wb_last%d" % h, [P, PACK, H // 2], F32) for h in range(2)]
+        w2_raw = [held("w2_raw%d" % h, [P, PACK, width], F32) for h, (c0, width) in enumerate(W2_PARTS)]
+        moved_sc = [held("moved_sc%d" % a, [P, S], U8) for a in range(1, PASSES)]
+        neg_y = [held("neg_y%d" % t, [P, LAYS + SPARE], F32) for t in range(PACK)]
+
+        nc.vector.memset(tab_sc[:].bitcast(I32), 0)
+        nc.vector.memset(wa_sc_raw[:].bitcast(I32), 0)
+        for plane in moved_sc:
+            nc.gpsimd.memset(plane[:].bitcast(I32), 0)
+        for t in range(PACK):
+            nc.gpsimd.memset(neg_y[t][:, LAYS:], 0.0)
+
+        warm = held("warm", [P, 16], F32)
+        nc.gpsimd.memset(warm[:, 0:1], 0.0)
+        nc.scalar.activation(warm[:, 8:9], warm[:, 0:1], ACT.Sin)
+        def load_tab(a, h, parts=2):
+            cols = slice(h * T // parts, (h + 1) * T // parts)
+            nc.sync.dma_start(tab[a][:, cols], tab_words[a].rearrange("p n i -> p (n i)").bitcast(I32)[:, cols])
+
+        def load_tab_scales(a, q):
+            nc.sync.dma_start(
+                tab_sc[32 * q + 4 * a : 32 * q + 4 * a + 4, :].bitcast(I32),
+                tab_scales[a, 4 * q : 4 * q + 4, :].bitcast(I32),
+            )
+
+        def load_rows(dst, w, a, cols):
+            nc.sync.dma_start(dst[:], w[512 * a : 512 * (a + 1), cols].rearrange("(p j) c -> p j c", j=PACK))
+
+        scale_rows = [(a, q) for a in range(PASSES) for q in range(4)]
+        load_tab(0, 0, 4)
+        nc.sync.dma_start(idx[:], offs)
+        for h in range(1, 4):
+            load_tab(0, h, 4)
+        nc.sync.dma_start(wa_raw[:].bitcast(I32), wa_words.rearrange("a p n -> p a n").bitcast(I32))
+        for j in range(2):
+            nc.sync.dma_start(
+                wb_raw[0][:, 2 * j : 2 * j + 2, :], wb[0:512, :].rearrange("(p j) c -> p j c", j=PACK)[:, 2 * j : 2 * j + 2, :]
+            )
+        for a, q in scale_rows[:6]:
+            load_tab_scales(a, q)
+        load_tab(1, 0)
+        for a, q in scale_rows[6:]:
+            load_tab_scales(a, q)
+        load_tab(1, 1)
+        for q in range(4):
+            nc.sync.dma_start(
+                wa_sc_raw[32 * q : 32 * q + 4, :, :].bitcast(I32),
+                wa_scales[:, 4 * q : 4 * q + 4, :].rearrange("a r n -> r a n").bitcast(I32),
+            )
+        load_rows(wb_raw[1], wb, 1, slice(0, H))
+        load_tab(2, 0)
+        load_tab(2, 1)
+        for h in range(2):
+            load_rows(wb_last[h], wb, PASSES - 1, slice(h * H // 2, (h + 1) * H // 2))
+        for h in range(2):
+            load_rows(w2_raw[h], w2, 0, slice(W2_PARTS[h][0], W2_PARTS[h][0] + W2_PARTS[h][1]))
+        nc.sync.dma_start(p1[:], pos1)
+        nc.sync.dma_start(p2[:], pos2)
+        nc.sync.dma_start(gain_sb[:], gain.rearrange("(p t) -> p t", t=PACK))
+        load_rows(w2_raw[2], w2, 0, slice(H // 2, H))
+        nc.sync.dma_start(p3[:], pos3)
+
+        wa_q = held("wa_q", [P, PASSES, 2 * H], U8)
+        wa_sc = held("wa_sc", [P, PASSES, H], U8)
+        nc.vector.tensor_copy(
+            wa_q[:].bitcast(U16).rearrange("p a (t m) -> p a t m", t=PACK),
+            wa_raw[:].bitcast(U16).rearrange("p a (m t) -> p a t m", t=PACK),
+        )
+
+        def round_and_deal(copy, dealt, raw, m0):
+            count = raw.shape[2] // PACK
+            copy(
+                dealt[:].rearrange("p (t m j) -> p m t j", t=PACK, j=PACK)[:, m0 : m0 + count],
+                raw[:].rearrange("p j (m t) -> p m t j", t=PACK),
+            )
+
+        picked = [[held("picked%d_%d" % (a, h), [P, BANK], U32) for h in range(HALVES)] for a in range(PASSES)]
+        picked_sc = held("picked_sc", [P, S], U8)
+
+        def gather_words(a):
+            for h in range(HALVES):
+                nc.vector.tensor_copy(picked[a][h][:], tab[a][:].bitcast(U32).indirect(idx[:, 32 * h : 32 * (h + 1)]))
+
+        wb_bf = [held("wb_bf%d" % a, [P, PACK * H], BF16) for a in range(PASSES)]
+        wb_q = [held("wb_q%d" % a, [P, H], U32) for a in range(PASSES)]
+        wb_sc = [held("wb_sc%d" % a, [P, H], U8) for a in range(PASSES)]
+
+        gather_words(0)
+        nc.vector.tensor_copy(picked_sc[:], tab_sc[:].indirect(idx[:]))
+        for a in range(1, PASSES):
+            nc.scalar.dma_start(moved_sc[a - 1][0:112, :].bitcast(I32), picked_sc[4 * a : 4 * a + 112, :].bitcast(I32))
+        nc.vector.tensor_copy(
+            wa_sc[:].rearrange("p a (t m) -> p a t m", t=PACK),
+            wa_sc_raw[:].rearrange("p a (m t) -> p a t m", t=PACK),
+        )
+        for a in range(PASSES - 1):
+            round_and_deal(nc.scalar.copy, wb_bf[a], wb_raw[a], 0)
+            nc.vector.quantize_mx(wb_q[a][:].bitcast(FP8X4), wb_sc[a][:], wb_bf[a][:])
+            gather_words(a + 1)
+        last = PASSES - 1
+        round_and_deal(nc.scalar.copy, wb_bf[last], wb_last[0], 0)
+        dealt_last = wb_bf[last][:].rearrange("p (t m j) -> p t m j", t=PACK, j=PACK)[:, :, P // 2 :, :]
+        raw_last = wb_last[1][:].rearrange("p j (m t) -> p t m j", t=PACK)
+        for t in range(2):
+            nc.vector.tensor_copy(dealt_last[:, t], raw_last[:, t])
+        nc.scalar.copy(
+            dealt_last[:, 2:].rearrange("p t m j -> p m t j"), raw_last[:, 2:].rearrange("p t m j -> p m t j")
+        )
+        for t in range(PACK):
+            nc.vector.quantize_mx(
+                wb_q[last][:, P * t : P * (t + 1)].bitcast(FP8X4),
+                wb_sc[last][:, P * t : P * (t + 1)],
+                wb_bf[last][:, PACK * P * t : PACK * P * (t + 1)],
+            )
+
+        w2_bf = held("w2_bf", [P, PACK * H], BF16)
+        w2_sc = held("w2_sc", [P, H], U8)
+
+        level = {}
+        phase = {}
+
+        def open_banks(t):
+            for h in range(HALVES):
+                phase[t, h] = psum.tile([P, BANK], F32, name="phase")
+                level[t, h] = psum.tile([P, BANK], F32, name="level")
+
+        def level_pass(t, h, a):
+            plane = picked_sc if a == 0 else moved_sc[a - 1]
+            nc.tensor.matmul_mx(
+                level[t, h][:],
+                lhsT=wa_q[:, a, 2 * P * t : 2 * P * (t + 1)].bitcast(FP4X4),
+                lhsT_scale=wa_sc[:, a, P * t : P * (t + 1)],
+                rhs=picked[a][h][:].bitcast(FP8X4),
+                rhs_scale=plane[:, BANK * h : BANK * (h + 1)],
+                start=(a == 0),
+                stop=(a == last),
+            )
+
+        def phase_pass(t, h, a):
+            nc.tensor.matmul_mx(
+                phase[t, h][:],
+                lhsT=wb_q[a][:, P * t : P * (t + 1)].bitcast(FP8X4),
+                lhsT_scale=wb_sc[a][:, P * t : P * (t + 1)],
+                rhs=picked[a][h][:].bitcast(FP8X4),
+                rhs_scale=picked_sc[4 * a :, BANK * h : BANK * (h + 1)],
+                start=(a == 0),
+                stop=(a == last),
+            )
+
+        hs = [held("hs%d" % t, [P, S], F32) for t in range(PACK)]
+        versine = {}
+
+        def sine(t):
+            for h in range(HALVES):
+                half_sine = ring.tile([P, BANK], F32, name="half_sine")
+                nc.scalar.activation(half_sine[:], phase[t, h][:], ACT.Sin, bias=-math.pi / 4, scale=0.5)
+                versine[t, h] = held("slot%d_%d" % (t, h), [P, BANK], F32)
+                if (t, h) == (0, 0):
+                    nc.vector.scalar_tensor_tensor(versine[t, h][:], half_sine[:], 2.0, half_sine[:], ALU.mult, ALU.mult)
+                else:
+                    nc.scalar.activation(versine[t, h][:], half_sine[:], ACT.Square, scale=math.sqrt(2.0))
+
+        def make_hs(t, h):
+            nc.vector.scalar_tensor_tensor(
+                hs[t][:, BANK * h : BANK * (h + 1)], level[t, h][:], 1.0, versine[t, h][:], ALU.add, ALU.subtract
+            )
+
+        pairs = [held("pairs%d" % c, [P, 2, 2 * width], BF16) for c, (m0, width) in enumerate(LAY_CHUNKS[:-1])]
+        diff_bf = [held("diff_bf%d" % c, [P, PACK * width], BF16) for c, (m0, width) in enumerate(LAY_CHUNKS)]
+
+        def first_pick(t, m0, width, first):
+            nc.vector.tensor_copy(first[:], hs[t][:].indirect(p1[:, m0 // 16 : (m0 + width) // 16]))
+            return first
+
+        def second_pick(t, m0, width, first, delta):
+            nc.vector.tensor_tensor(
+                delta[:], hs[t][:].indirect(p2[:, m0 // 16 : (m0 + width) // 16]), first[:], ALU.subtract
+            )
+            return delta
+
+        def round_diff(t, c, delta_cols):
+            dst = pairs[c][:, t // 2, t % 2 :: 2] if c < len(pairs) else diff_bf[c][:, t::PACK]
+            nc.scalar.activation(dst, delta_cols, ACT.Abs, scale=gain_sb[:, t : t + 1])
+
+        for t in range(2):
+            open_banks(t)
+        for a in range(PASSES):
+            for t in range(2):
+                for h in range(HALVES):
+                    level_pass(t, h, a)
+            for t in range(2):
+                for h in range(HALVES):
+                    phase_pass(t, h, a)
+        for h in range(2):
+            round_and_deal(nc.vector.tensor_copy, w2_bf, w2_raw[h], W2_PARTS[h][0] // PACK)
+        sine(0)
+        make_hs(0, 0)
+        make_hs(0, 1)
+        sine(1)
+        for t in range(2):
+            open_banks(t + 2)
+            for h in range(HALVES):
+                for a in range(PASSES):
+                    phase_pass(t + 2, h, a)
+            for h in range(HALVES):
+                for a in range(PASSES):
+                    level_pass(t + 2, h, a)
+            sine(t + 2)
+        first = first_pick(0, 0, LAYS, held("first0", [P, LAYS], F32))
+        make_hs(1, 0)
+        deltas = [second_pick(0, 0, LAYS, first, held("slot1_0", [P, LAYS], F32))]
+        make_hs(1, 1)
+        make_hs(2, 0)
+        first = first_pick(1, 0, LAYS, held("slot2_0", [P, LAYS], F32))
+        make_hs(2, 1)
+        deltas.append(second_pick(1, 0, LAYS, first, held("slot2_1", [P, LAYS], F32)))
+        make_hs(3, 0)
+        make_hs(3, 1)
+        for t in range(2):
+            for c, (m0, width) in enumerate(LAY_CHUNKS):
+                round_diff(t, c, deltas[t][:, m0 : m0 + width])
+        round_and_deal(nc.scalar.copy, w2_bf, w2_raw[2], P // 2)
+        w2_q_first = held("w2_q_first", [P, P], U32)
+        nc.vector.quantize_mx(w2_q_first[:].bitcast(FP8X4), w2_sc[:, 0:P], w2_bf[:, 0 : PACK * P])
+
+        y_first = [psum.tile([P, BANK], F32, name="phase") for c in range(len(LAY_CHUNKS))]
+        y_rest = [psum.tile([P, BANK], F32, name="level") for t in range(1, PACK)]
+        diff_q = []
+        for c, (m0, width) in enumerate(LAY_CHUNKS):
+            firsts = [first_pick(t, m0, width, held("slot3_%d" % (3 - t), [P, width], F32)) for t in (2, 3)]
+            for t in (2, 3):
+                delta = second_pick(t, m0, width, firsts[t - 2], ring.tile([P, width], F32, name="delta"))
+                round_diff(t, c, delta[:])
+            if c < len(pairs):
+                nc.scalar.copy(
+                    diff_bf[c][:].bitcast(F32).rearrange("p (m u) -> p m u", u=2),
+                    pairs[c][:].bitcast(F32).rearrange("p u m -> p m u"),
+                )
+        for c, (m0, width) in enumerate(LAY_CHUNKS):
+            codes = held("diff_q%d" % c, [P, width], U32)
+            scales = held("diff_sc%d" % c, [P, width], U8)
+            nc.vector.quantize_mx(codes[:].bitcast(FP8X4), scales[:], diff_bf[c][:])
+            diff_q.append((codes, scales))
+
+        w2_q = [w2_q_first[:]]
+
+        def second_stage(bank, t, c):
+            nc.tensor.matmul_mx(
+                bank,
+                lhsT=w2_q[t].bitcast(FP8X4),
+                lhsT_scale=w2_sc[:, P * t : P * (t + 1)],
+                rhs=diff_q[c][0][:].bitcast(FP8X4),
+                rhs_scale=diff_q[c][1][:],
+                start=True,
+                stop=True,
+            )
+
+        for c, (m0, width) in enumerate(LAY_CHUNKS):
+            second_stage(y_first[c][:, 0:width], 0, c)
+            nc.scalar.activation(neg_y[0][:, m0 : m0 + width], y_first[c][:, 0:width], ACT.Copy, scale=-1.0)
+
+        out_rows = out.rearrange("(p t) j -> p t j", t=PACK)
+
+        def finish(t, j0, width, square):
+            score = held("score%d_%d" % (t, j0), [P, width], F32)
+            nc.vector.tensor_tensor(
+                score[:], neg_y[t][:].indirect(p3[:, j0 // 16 : (j0 + width) // 16]), square[:], ALU.add
+            )
+            nc.sync.dma_start(out_rows[:, t, j0 : j0 + width], score[:])
+
+        square = held("diff_bf2", [P, BANK], F32)
+        nc.vector.tensor_tensor(square[:], hs[0][:, 0:BANK], hs[0][:, 0:BANK], ALU.mult)
+        finish(0, 0, BANK, square)
+        w2_q_rest = held("diff_bf2", [P, H - P], U32)
+        nc.vector.quantize_mx(w2_q_rest[:, 0:P].bitcast(FP8X4), w2_sc[:, P : 2 * P], w2_bf[:, PACK * P : 2 * PACK * P])
+        nc.vector.quantize_mx(w2_q_rest[:, P:].bitcast(FP8X4), w2_sc[:, 2 * P :], w2_bf[:, 2 * PACK * P :])
+        w2_q.extend(w2_q_rest[:, P * t : P * (t + 1)] for t in range(PACK - 1))
+        for t in range(1, PACK):
+            for c, (m0, width) in enumerate(LAY_CHUNKS):
+                second_stage(y_rest[t - 1][:, m0 : m0 + width], t, c)
+        for t in range(PACK):
+            if t > 0:
+                nc.scalar.activation(neg_y[t][:, 0:LAYS], y_rest[t - 1][:], ACT.Copy, scale=-1.0)
+            pieces = ((0, 512), (512, 512)) if t < PACK - 1 else ((0, 512), (512, 256), (768, 256))
+            for j0, width in pieces[1:] if t == 0 else pieces:
+                square = held("square%d_%d" % (t, j0), [P, width], F32)
+                nc.scalar.activation(square[:], hs[t][:, j0 : j0 + width], ACT.Square)
+                finish(t, j0, width, square)

@@ -24,6 +24,7 @@ BANK = 512
 HALVES = S // BANK
 SPARE = 16
 W2_PARTS = ((0, 128), (128, 128), (256, 256))
+SPREAD = (0, 4, 1)
 LAY_CHUNKS = ((0, 256), (256, 128), (384, 128))
 
 
@@ -50,8 +51,8 @@ def tile_list_rope_lay_anomaly_kernel(
         wa_sc_raw = held("wa_sc_raw", [P, PASSES, H], U8)
         wb_raw = [held("wb_raw%d" % a, [P, PACK, H], F32) for a in range(PASSES - 1)]
         wb_last = [held("wb_last%d" % h, [P, PACK, H // 2], F32) for h in range(2)]
-        w2_raw = [held("w2_raw%d" % h, [P, PACK, width], F32) for h, (c0, width) in enumerate(W2_PARTS)]
-        moved_sc = [held("moved_sc%d" % a, [P, S], U8) for a in range(1, PASSES)]
+        w2_raw = [held("w2_raw%d" % h, [P, PACK, width], F32) for h, (c0, width) in enumerate(W2_PARTS[:2])]
+        moved_sc = [held("moved_sc%d" % a, [P, S], U8) for a in range(PASSES)]
         neg_y = [held("neg_y%d" % t, [P, LAYS + SPARE], F32) for t in range(PACK)]
 
         nc.vector.memset(tab_sc[:].bitcast(I32), 0)
@@ -68,36 +69,28 @@ def tile_list_rope_lay_anomaly_kernel(
             cols = slice(h * T // parts, (h + 1) * T // parts)
             nc.sync.dma_start(tab[a][:, cols], tab_words[a].rearrange("p n i -> p (n i)").bitcast(I32)[:, cols])
 
-        def load_tab_scales(a, q):
-            nc.sync.dma_start(
-                tab_sc[32 * q + 4 * a : 32 * q + 4 * a + 4, :].bitcast(I32),
-                tab_scales[a, 4 * q : 4 * q + 4, :].bitcast(I32),
-            )
+        def load_tab_scales(a):
+            nc.sync.dma_start(tab_sc[SPREAD[a] : P : 8, :].bitcast(I32), tab_scales[a].bitcast(I32))
 
         def load_rows(dst, w, a, cols):
             nc.sync.dma_start(dst[:], w[512 * a : 512 * (a + 1), cols].rearrange("(p j) c -> p j c", j=PACK))
 
-        scale_rows = [(a, q) for a in range(PASSES) for q in range(4)]
         load_tab(0, 0, 4)
         nc.sync.dma_start(idx[:], offs)
         for h in range(1, 4):
             load_tab(0, h, 4)
-        nc.sync.dma_start(wa_raw[:].bitcast(I32), wa_words.rearrange("a p n -> p a n").bitcast(I32))
-        for j in range(2):
+        for a in range(PASSES):
+            nc.sync.dma_start(wa_raw[:, a, :].bitcast(I32), wa_words[a].bitcast(I32))
+        for a in range(PASSES):
+            load_tab_scales(a)
+        load_rows(wb_raw[0], wb, 0, slice(0, H))
+        for r in range(4):
             nc.sync.dma_start(
-                wb_raw[0][:, 2 * j : 2 * j + 2, :], wb[0:512, :].rearrange("(p j) c -> p j c", j=PACK)[:, 2 * j : 2 * j + 2, :]
+                wa_sc_raw[r:P:32, :, :].bitcast(I32),
+                wa_scales[:, r:16:4, :].rearrange("a q n -> q a n").bitcast(I32),
             )
-        for a, q in scale_rows[:6]:
-            load_tab_scales(a, q)
         load_tab(1, 0)
-        for a, q in scale_rows[6:]:
-            load_tab_scales(a, q)
         load_tab(1, 1)
-        for q in range(4):
-            nc.sync.dma_start(
-                wa_sc_raw[32 * q : 32 * q + 4, :, :].bitcast(I32),
-                wa_scales[:, 4 * q : 4 * q + 4, :].rearrange("a r n -> r a n").bitcast(I32),
-            )
         load_rows(wb_raw[1], wb, 1, slice(0, H))
         load_tab(2, 0)
         load_tab(2, 1)
@@ -108,7 +101,6 @@ def tile_list_rope_lay_anomaly_kernel(
         nc.sync.dma_start(p1[:], pos1)
         nc.sync.dma_start(p2[:], pos2)
         nc.sync.dma_start(gain_sb[:], gain.rearrange("(p t) -> p t", t=PACK))
-        load_rows(w2_raw[2], w2, 0, slice(H // 2, H))
         nc.sync.dma_start(p3[:], pos3)
 
         wa_q = held("wa_q", [P, PASSES, 2 * H], U8)
@@ -136,10 +128,13 @@ def tile_list_rope_lay_anomaly_kernel(
         wb_q = [held("wb_q%d" % a, [P, H], U32) for a in range(PASSES)]
         wb_sc = [held("wb_sc%d" % a, [P, H], U8) for a in range(PASSES)]
 
-        gather_words(0)
         nc.vector.tensor_copy(picked_sc[:], tab_sc[:].indirect(idx[:]))
-        for a in range(1, PASSES):
-            nc.scalar.dma_start(moved_sc[a - 1][0:112, :].bitcast(I32), picked_sc[4 * a : 4 * a + 112, :].bitcast(I32))
+        for a in range(PASSES):
+            for r in range(4):
+                nc.gpsimd.dma_start(
+                    moved_sc[a][r:P:32, :].bitcast(I32), picked_sc[8 * r + SPREAD[a] : P : 32, :].bitcast(I32)
+                )
+        gather_words(0)
         nc.vector.tensor_copy(
             wa_sc[:].rearrange("p a (t m) -> p a t m", t=PACK),
             wa_sc_raw[:].rearrange("p a (m t) -> p a t m", t=PACK),
@@ -176,13 +171,12 @@ def tile_list_rope_lay_anomaly_kernel(
                 level[t, h] = psum.tile([P, BANK], F32, name="level")
 
         def level_pass(t, h, a):
-            plane = picked_sc if a == 0 else moved_sc[a - 1]
             nc.tensor.matmul_mx(
                 level[t, h][:],
                 lhsT=wa_q[:, a, 2 * P * t : 2 * P * (t + 1)].bitcast(FP4X4),
                 lhsT_scale=wa_sc[:, a, P * t : P * (t + 1)],
                 rhs=picked[a][h][:].bitcast(FP8X4),
-                rhs_scale=plane[:, BANK * h : BANK * (h + 1)],
+                rhs_scale=moved_sc[a][:, BANK * h : BANK * (h + 1)],
                 start=(a == 0),
                 stop=(a == last),
             )
@@ -193,7 +187,7 @@ def tile_list_rope_lay_anomaly_kernel(
                 lhsT=wb_q[a][:, P * t : P * (t + 1)].bitcast(FP8X4),
                 lhsT_scale=wb_sc[a][:, P * t : P * (t + 1)],
                 rhs=picked[a][h][:].bitcast(FP8X4),
-                rhs_scale=picked_sc[4 * a :, BANK * h : BANK * (h + 1)],
+                rhs_scale=moved_sc[a][:, BANK * h : BANK * (h + 1)],
                 start=(a == 0),
                 stop=(a == last),
             )
@@ -203,7 +197,10 @@ def tile_list_rope_lay_anomaly_kernel(
 
         def sine(t):
             for h in range(HALVES):
-                half_sine = ring.tile([P, BANK], F32, name="half_sine")
+                if (t, h) == (2, 1):
+                    half_sine = held("late_w2", [P, BANK], F32)
+                else:
+                    half_sine = ring.tile([P, BANK], F32, name="half_sine")
                 nc.scalar.activation(half_sine[:], phase[t, h][:], ACT.Sin, bias=-math.pi / 4, scale=0.5)
                 versine[t, h] = held("slot%d_%d" % (t, h), [P, BANK], F32)
                 if (t, h) == (0, 0):
@@ -270,7 +267,9 @@ def tile_list_rope_lay_anomaly_kernel(
         for t in range(2):
             for c, (m0, width) in enumerate(LAY_CHUNKS):
                 round_diff(t, c, deltas[t][:, m0 : m0 + width])
-        round_and_deal(nc.scalar.copy, w2_bf, w2_raw[2], P // 2)
+        w2_late = held("late_w2", [P, PACK, H // 2], F32)
+        load_rows(w2_late, w2, 0, slice(H // 2, H))
+        round_and_deal(nc.scalar.copy, w2_bf, w2_late, P // 2)
         w2_q_first = held("w2_q_first", [P, P], U32)
         nc.vector.quantize_mx(w2_q_first[:].bitcast(FP8X4), w2_sc[:, 0:P], w2_bf[:, 0 : PACK * P])
 
@@ -313,7 +312,7 @@ def tile_list_rope_lay_anomaly_kernel(
         out_rows = out.rearrange("(p t) j -> p t j", t=PACK)
 
         def finish(t, j0, width, square):
-            score = held("score%d_%d" % (t, j0), [P, width], F32)
+            score = held("w2_bf" if (t, j0) == (0, BANK) else "score%d_%d" % (t, j0), [P, width], F32)
             nc.vector.tensor_tensor(
                 score[:], neg_y[t][:].indirect(p3[:, j0 // 16 : (j0 + width) // 16]), square[:], ALU.add
             )

@@ -75,14 +75,18 @@ def tile_list_rope_lay_anomaly_kernel(
         def load_rows(dst, w, a, cols):
             nc.sync.dma_start(dst[:], w[512 * a : 512 * (a + 1), cols].rearrange("(p j) c -> p j c", j=PACK))
 
-        load_tab(0, 0, 4)
         nc.sync.dma_start(idx[:], offs)
-        for h in range(1, 4):
-            load_tab(0, h, 4)
-        for a in range(PASSES):
-            nc.sync.dma_start(wa_raw[:, a, :].bitcast(I32), wa_words[a].bitcast(I32))
+        load_tab(0, 0, 4)
+        nc.sync.dma_start(p1[:], pos1)
+        nc.sync.dma_start(p2[:], pos2)
+        load_tab(0, 1, 4)
+        nc.sync.dma_start(p3[:], pos3)
+        nc.sync.dma_start(gain_sb[:], gain.rearrange("(p t) -> p t", t=PACK))
+        load_tab(0, 2, 4)
         for a in range(PASSES):
             load_tab_scales(a)
+        load_tab(0, 3, 4)
+        nc.sync.dma_start(wa_raw[:].bitcast(I32), wa_words.rearrange("a p n -> p a n").bitcast(I32))
         load_rows(wb_raw[0], wb, 0, slice(0, H))
         for r in range(4):
             nc.sync.dma_start(
@@ -98,10 +102,6 @@ def tile_list_rope_lay_anomaly_kernel(
             load_rows(wb_last[h], wb, PASSES - 1, slice(h * H // 2, (h + 1) * H // 2))
         for h in range(2):
             load_rows(w2_raw[h], w2, 0, slice(W2_PARTS[h][0], W2_PARTS[h][0] + W2_PARTS[h][1]))
-        nc.sync.dma_start(p1[:], pos1)
-        nc.sync.dma_start(p2[:], pos2)
-        nc.sync.dma_start(gain_sb[:], gain.rearrange("(p t) -> p t", t=PACK))
-        nc.sync.dma_start(p3[:], pos3)
 
         wa_q = held("wa_q", [P, PASSES, 2 * H], U8)
         wa_sc = held("wa_sc", [P, PASSES, H], U8)
@@ -152,14 +152,17 @@ def tile_list_rope_lay_anomaly_kernel(
         nc.scalar.copy(
             dealt_last[:, 2:].rearrange("p t m j -> p m t j"), raw_last[:, 2:].rearrange("p t m j -> p m t j")
         )
+        w2_bf = held("w2_bf", [P, PACK * H], BF16)
         for t in range(PACK):
+            if t == 2:
+                for h in range(2):
+                    round_and_deal(nc.vector.tensor_copy, w2_bf, w2_raw[h], W2_PARTS[h][0] // PACK)
             nc.vector.quantize_mx(
                 wb_q[last][:, P * t : P * (t + 1)].bitcast(FP8X4),
                 wb_sc[last][:, P * t : P * (t + 1)],
                 wb_bf[last][:, PACK * P * t : PACK * P * (t + 1)],
             )
 
-        w2_bf = held("w2_bf", [P, PACK * H], BF16)
         w2_sc = held("w2_sc", [P, H], U8)
 
         level = {}
@@ -232,15 +235,19 @@ def tile_list_rope_lay_anomaly_kernel(
 
         for t in range(2):
             open_banks(t)
-        for a in range(PASSES):
+        for a in range(last):
             for t in range(2):
                 for h in range(HALVES):
                     level_pass(t, h, a)
             for t in range(2):
                 for h in range(HALVES):
                     phase_pass(t, h, a)
-        for h in range(2):
-            round_and_deal(nc.vector.tensor_copy, w2_bf, w2_raw[h], W2_PARTS[h][0] // PACK)
+        level_pass(0, 0, last)
+        level_pass(1, 0, last)
+        for t in range(2):
+            level_pass(t, 1, last)
+            for h in range(HALVES):
+                phase_pass(t, h, last)
         sine(0)
         make_hs(0, 0)
         make_hs(0, 1)

import math
from contextlib import ExitStack

import concourse.mybir as mybir

K, H, T, S, LAYS = 1536, 512, 4096, 1024, 512
FLOPS = 2 * (2 * K * H * S + H * H * LAYS)

F32 = mybir.dt.float32
BF16 = mybir.dt.bfloat16
I32 = mybir.dt.int32
U32 = mybir.dt.uint32
U16 = mybir.dt.uint16
U8 = mybir.dt.uint8
FP8X4 = mybir.dt.float8_e4m3fn_x4
FP4X4 = mybir.dt.float4_e2m1fn_x4
ACT = mybir.ActivationFunctionType
ALU = mybir.AluOpType

P = 128
PACK = 4
PASSES = K // (P * PACK)
BANK = 512
HALVES = S // BANK
SPARE = 16
W2_PARTS = ((0, 128), (128, 128), (256, 256))
SPREAD = (0, 4, 1)
LAY_CHUNKS = ((0, 256), (256, 128), (384, 128))


def tile_list_rope_lay_anomaly_kernel(
    tc, tab_words, tab_scales, offs, pos1, pos2, pos3, wa_words, wa_scales, wb, gain, w2, out
):
    nc = tc.nc
    with ExitStack() as ctx:
        keep = ctx.enter_context(tc.tile_pool(name="keep", bufs=1))
        ring = ctx.enter_context(tc.tile_pool(name="ring", bufs=4))
        psum = ctx.enter_context(tc.psum_pool(name="psum", bufs=4))

        def held(name, shape, dtype):
            return keep.tile(shape, dtype, name=name, align_bytes=64)

        idx = keep.tile([P, S // 16], U16, name="idx")
        p1 = keep.tile([P, LAYS // 16], U16, name="p1")
        p2 = keep.tile([P, LAYS // 16], U16, name="p2")
        p3 = keep.tile([P, S // 16], U16, name="p3")
        gain_sb = held("gain_sb", [P, PACK], F32)
        tab = [held("tab%d" % a, [P, T], I32) for a in range(PASSES)]
        tab_sc = held("tab_sc", [P, T], U8)
        wa_raw = held("wa_raw", [P, PASSES, 2 * H], U8)
        wa_sc_raw = held("wa_sc_raw", [P, PASSES, H], U8)
        wb_raw = [held("wb_raw%d" % a, [P, PACK, H], F32) for a in range(PASSES - 1)]
        wb_last = [held("wb_last%d" % h, [P, PACK, H // 2], F32) for h in range(2)]
        w2_raw = [held("w2_raw%d" % h, [P, PACK, width], F32) for h, (c0, width) in enumerate(W2_PARTS[:2])]
        moved_sc = [held("moved_sc%d" % a, [P, S], U8) for a in range(PASSES)]
        neg_y = [held("neg_y%d" % t, [P, LAYS + SPARE], F32) for t in range(PACK)]

        nc.vector.memset(tab_sc[:].bitcast(I32), 0)
        nc.vector.memset(wa_sc_raw[:].bitcast(I32), 0)
        for plane in moved_sc:
            nc.gpsimd.memset(plane[:].bitcast(I32), 0)
        for t in range(PACK):
            nc.gpsimd.memset(neg_y[t][:, LAYS:], 0.0)

        warm = held("warm", [P, 16], F32)
        nc.gpsimd.memset(warm[:, 0:1], 0.0)
        nc.scalar.activation(warm[:, 8:9], warm[:, 0:1], ACT.Sin)
        def load_tab(a, h, parts=2):
            cols = slice(h * T // parts, (h + 1) * T // parts)
            nc.sync.dma_start(tab[a][:, cols], tab_words[a].rearrange("p n i -> p (n i)").bitcast(I32)[:, cols])

        def load_tab_scales(a):
            nc.sync.dma_start(tab_sc[SPREAD[a] : P : 8, :].bitcast(I32), tab_scales[a].bitcast(I32))

        def load_rows(dst, w, a, cols):
            nc.sync.dma_start(dst[:], w[512 * a : 512 * (a + 1), cols].rearrange("(p j) c -> p j c", j=PACK))

        nc.sync.dma_start(idx[:], offs)
        load_tab(0, 0, 4)
        nc.sync.dma_start(p1[:], pos1)
        nc.sync.dma_start(p2[:], pos2)
        load_tab(0, 1, 4)
        nc.sync.dma_start(p3[:], pos3)
        nc.sync.dma_start(gain_sb[:], gain.rearrange("(p t) -> p t", t=PACK))
        load_tab(0, 2, 4)
        for a in range(PASSES):
            load_tab_scales(a)
        load_tab(0, 3, 4)
        nc.sync.dma_start(wa_raw[:].bitcast(I32), wa_words.rearrange("a p n -> p a n").bitcast(I32))
        load_rows(wb_raw[0], wb, 0, slice(0, H))
        for r in range(4):
            nc.sync.dma_start(
                wa_sc_raw[r:P:32, :, :].bitcast(I32),
                wa_scales[:, r:16:4, :].rearrange("a q n -> q a n").bitcast(I32),
            )
        load_tab(1, 0)
        load_tab(1, 1)
        load_rows(wb_raw[1], wb, 1, slice(0, H))
        load_tab(2, 0)
        load_tab(2, 1)
        for h in range(2):
            load_rows(wb_last[h], wb, PASSES - 1, slice(h * H // 2, (h + 1) * H // 2))
        for h in range(2):
            load_rows(w2_raw[h], w2, 0, slice(W2_PARTS[h][0], W2_PARTS[h][0] + W2_PARTS[h][1]))

        wa_q = held("wa_q", [P, PASSES, 2 * H], U8)
        wa_sc = held("wa_sc", [P, PASSES, H], U8)
        nc.vector.tensor_copy(
            wa_q[:].bitcast(U16).rearrange("p a (t m) -> p a t m", t=PACK),
            wa_raw[:].bitcast(U16).rearrange("p a (m t) -> p a t m", t=PACK),
        )

        def round_and_deal(copy, dealt, raw, m0):
            count = raw.shape[2] // PACK
            copy(
                dealt[:].rearrange("p (t m j) -> p m t j", t=PACK, j=PACK)[:, m0 : m0 + count],
                raw[:].rearrange("p j (m t) -> p m t j", t=PACK),
            )

        picked = [[held("picked%d_%d" % (a, h), [P, BANK], U32) for h in range(HALVES)] for a in range(PASSES)]
        picked_sc = held("picked_sc", [P, S], U8)

        def gather_words(a):
            for h in range(HALVES):
                nc.vector.tensor_copy(picked[a][h][:], tab[a][:].bitcast(U32).indirect(idx[:, 32 * h : 32 * (h + 1)]))

        wb_bf = [held("wb_bf%d" % a, [P, PACK * H], BF16) for a in range(PASSES)]
        wb_q = [held("wb_q%d" % a, [P, H], U32) for a in range(PASSES)]
        wb_sc = [held("wb_sc%d" % a, [P, H], U8) for a in range(PASSES)]

        nc.vector.tensor_copy(picked_sc[:], tab_sc[:].indirect(idx[:]))
        for a in range(PASSES):
            for r in range(4):
                nc.gpsimd.dma_start(
                    moved_sc[a][r:P:32, :].bitcast(I32), picked_sc[8 * r + SPREAD[a] : P : 32, :].bitcast(I32)
                )
        gather_words(0)
        nc.vector.tensor_copy(
            wa_sc[:].rearrange("p a (t m) -> p a t m", t=PACK),
            wa_sc_raw[:].rearrange("p a (m t) -> p a t m", t=PACK),
        )
        for a in range(PASSES - 1):
            round_and_deal(nc.scalar.copy, wb_bf[a], wb_raw[a], 0)
            nc.vector.quantize_mx(wb_q[a][:].bitcast(FP8X4), wb_sc[a][:], wb_bf[a][:])
            gather_words(a + 1)
        last = PASSES - 1
        round_and_deal(nc.scalar.copy, wb_bf[last], wb_last[0], 0)
        dealt_last = wb_bf[last][:].rearrange("p (t m j) -> p t m j", t=PACK, j=PACK)[:, :, P // 2 :, :]
        raw_last = wb_last[1][:].rearrange("p j (m t) -> p t m j", t=PACK)
        for t in range(2):
            nc.vector.tensor_copy(dealt_last[:, t], raw_last[:, t])
        nc.scalar.copy(
            dealt_last[:, 2:].rearrange("p t m j -> p m t j"), raw_last[:, 2:].rearrange("p t m j -> p m t j")
        )
        w2_bf = held("w2_bf", [P, PACK * H], BF16)
        for t in range(PACK):
            if t == 2:
                for h in range(2):
                    round_and_deal(nc.vector.tensor_copy, w2_bf, w2_raw[h], W2_PARTS[h][0] // PACK)
            nc.vector.quantize_mx(
                wb_q[last][:, P * t : P * (t + 1)].bitcast(FP8X4),
                wb_sc[last][:, P * t : P * (t + 1)],
                wb_bf[last][:, PACK * P * t : PACK * P * (t + 1)],
            )

        w2_sc = held("w2_sc", [P, H], U8)

        level = {}
        phase = {}

        def open_banks(t):
            for h in range(HALVES):
                phase[t, h] = psum.tile([P, BANK], F32, name="phase")
                level[t, h] = psum.tile([P, BANK], F32, name="level")

        def level_pass(t, h, a):
            nc.tensor.matmul_mx(
                level[t, h][:],
                lhsT=wa_q[:, a, 2 * P * t : 2 * P * (t + 1)].bitcast(FP4X4),
                lhsT_scale=wa_sc[:, a, P * t : P * (t + 1)],
                rhs=picked[a][h][:].bitcast(FP8X4),
                rhs_scale=moved_sc[a][:, BANK * h : BANK * (h + 1)],
                start=(a == 0),
                stop=(a == last),
            )

        def phase_pass(t, h, a):
            nc.tensor.matmul_mx(
                phase[t, h][:],
                lhsT=wb_q[a][:, P * t : P * (t + 1)].bitcast(FP8X4),
                lhsT_scale=wb_sc[a][:, P * t : P * (t + 1)],
                rhs=picked[a][h][:].bitcast(FP8X4),
                rhs_scale=moved_sc[a][:, BANK * h : BANK * (h + 1)],
                start=(a == 0),
                stop=(a == last),
            )

        hs = [held("hs%d" % t, [P, S], F32) for t in range(PACK)]
        versine = {}

        def sine(t):
            for h in range(HALVES):
                if (t, h) == (2, 1):
                    half_sine = held("late_w2", [P, BANK], F32)
                else:
                    half_sine = ring.tile([P, BANK], F32, name="half_sine")
                nc.scalar.activation(half_sine[:], phase[t, h][:], ACT.Sin, bias=-math.pi / 4, scale=0.5)
                versine[t, h] = held("slot%d_%d" % (t, h), [P, BANK], F32)
                if (t, h) == (0, 0):
                    nc.vector.scalar_tensor_tensor(versine[t, h][:], half_sine[:], 2.0, half_sine[:], ALU.mult, ALU.mult)
                else:
                    nc.scalar.activation(versine[t, h][:], half_sine[:], ACT.Square, scale=math.sqrt(2.0))

        def make_hs(t, h):
            nc.vector.scalar_tensor_tensor(
                hs[t][:, BANK * h : BANK * (h + 1)], level[t, h][:], 1.0, versine[t, h][:], ALU.add, ALU.subtract
            )

        pairs = [held("pairs%d" % c, [P, 2, 2 * width], BF16) for c, (m0, width) in enumerate(LAY_CHUNKS[:-1])]
        diff_bf = [held("diff_bf%d" % c, [P, PACK * width], BF16) for c, (m0, width) in enumerate(LAY_CHUNKS)]

        def first_pick(t, m0, width, first):
            nc.vector.tensor_copy(first[:], hs[t][:].indirect(p1[:, m0 // 16 : (m0 + width) // 16]))
            return first

        def second_pick(t, m0, width, first, delta):
            nc.vector.tensor_tensor(
                delta[:], hs[t][:].indirect(p2[:, m0 // 16 : (m0 + width) // 16]), first[:], ALU.subtract
            )
            return delta

        def round_diff(t, c, delta_cols):
            dst = pairs[c][:, t // 2, t % 2 :: 2] if c < len(pairs) else diff_bf[c][:, t::PACK]
            nc.scalar.activation(dst, delta_cols, ACT.Abs, scale=gain_sb[:, t : t + 1])

        for t in range(2):
            open_banks(t)
        for a in range(last):
            for t in range(2):
                for h in range(HALVES):
                    level_pass(t, h, a)
            for t in range(2):
                for h in range(HALVES):
                    phase_pass(t, h, a)
        level_pass(0, 0, last)
        level_pass(1, 0, last)
        for t in range(2):
            level_pass(t, 1, last)
            for h in range(HALVES):
                phase_pass(t, h, last)
        sine(0)
        make_hs(0, 0)
        make_hs(0, 1)
        sine(1)
        for t in range(2):
            open_banks(t + 2)
            for h in range(HALVES):
                for a in range(PASSES):
                    phase_pass(t + 2, h, a)
            for h in range(HALVES):
                for a in range(PASSES):
                    level_pass(t + 2, h, a)
            sine(t + 2)
        first = first_pick(0, 0, LAYS, held("first0", [P, LAYS], F32))
        make_hs(1, 0)
        deltas = [second_pick(0, 0, LAYS, first, held("slot1_0", [P, LAYS], F32))]
        make_hs(1, 1)
        make_hs(2, 0)
        first = first_pick(1, 0, LAYS, held("slot2_0", [P, LAYS], F32))
        make_hs(2, 1)
        deltas.append(second_pick(1, 0, LAYS, first, held("slot2_1", [P, LAYS], F32)))
        make_hs(3, 0)
        make_hs(3, 1)
        for t in range(2):
            for c, (m0, width) in enumerate(LAY_CHUNKS):
                round_diff(t, c, deltas[t][:, m0 : m0 + width])
        w2_late = held("late_w2", [P, PACK, H // 2], F32)
        load_rows(w2_late, w2, 0, slice(H // 2, H))
        round_and_deal(nc.scalar.copy, w2_bf, w2_late, P // 2)
        w2_q_first = held("w2_q_first", [P, P], U32)
        nc.vector.quantize_mx(w2_q_first[:].bitcast(FP8X4), w2_sc[:, 0:P], w2_bf[:, 0 : PACK * P])

        y_first = [psum.tile([P, BANK], F32, name="phase") for c in range(len(LAY_CHUNKS))]
        y_rest = [psum.tile([P, BANK], F32, name="level") for t in range(1, PACK)]
        diff_q = []
        for c, (m0, width) in enumerate(LAY_CHUNKS):
            firsts = [first_pick(t, m0, width, held("slot3_%d" % (3 - t), [P, width], F32)) for t in (2, 3)]
            for t in (2, 3):
                delta = second_pick(t, m0, width, firsts[t - 2], ring.tile([P, width], F32, name="delta"))
                round_diff(t, c, delta[:])
            if c < len(pairs):
                nc.scalar.copy(
                    diff_bf[c][:].bitcast(F32).rearrange("p (m u) -> p m u", u=2),
                    pairs[c][:].bitcast(F32).rearrange("p u m -> p m u"),
                )
        for c, (m0, width) in enumerate(LAY_CHUNKS):
            codes = held("diff_q%d" % c, [P, width], U32)
            scales = held("diff_sc%d" % c, [P, width], U8)
            nc.vector.quantize_mx(codes[:].bitcast(FP8X4), scales[:], diff_bf[c][:])
            diff_q.append((codes, scales))

        w2_q = [w2_q_first[:]]

        def second_stage(bank, t, c):
            nc.tensor.matmul_mx(
                bank,
                lhsT=w2_q[t].bitcast(FP8X4),
                lhsT_scale=w2_sc[:, P * t : P * (t + 1)],
                rhs=diff_q[c][0][:].bitcast(FP8X4),
                rhs_scale=diff_q[c][1][:],
                start=True,
                stop=True,
            )

        for c, (m0, width) in enumerate(LAY_CHUNKS):
            second_stage(y_first[c][:, 0:width], 0, c)
            nc.scalar.activation(neg_y[0][:, m0 : m0 + width], y_first[c][:, 0:width], ACT.Copy, scale=-1.0)

        out_rows = out.rearrange("(p t) j -> p t j", t=PACK)

        def finish(t, j0, width, square):
            score = held("w2_bf" if (t, j0) == (0, BANK) else "score%d_%d" % (t, j0), [P, width], F32)
            nc.vector.tensor_tensor(
                score[:], neg_y[t][:].indirect(p3[:, j0 // 16 : (j0 + width) // 16]), square[:], ALU.add
            )
            nc.sync.dma_start(out_rows[:, t, j0 : j0 + width], score[:])

        square = held("diff_bf2", [P, BANK], F32)
        nc.vector.tensor_tensor(square[:], hs[0][:, 0:BANK], hs[0][:, 0:BANK], ALU.mult)
        finish(0, 0, BANK, square)
        w2_q_rest = held("diff_bf2", [P, H - P], U32)
        nc.vector.quantize_mx(w2_q_rest[:, 0:P].bitcast(FP8X4), w2_sc[:, P : 2 * P], w2_bf[:, PACK * P : 2 * PACK * P])
        nc.vector.quantize_mx(w2_q_rest[:, P:].bitcast(FP8X4), w2_sc[:, 2 * P :], w2_bf[:, 2 * PACK * P :])
        w2_q.extend(w2_q_rest[:, P * t : P * (t + 1)] for t in range(PACK - 1))
        for t in range(1, PACK):
            for c, (m0, width) in enumerate(LAY_CHUNKS):
                second_stage(y_rest[t - 1][:, m0 : m0 + width], t, c)
        for t in range(PACK):
            if t > 0:
                nc.scalar.activation(neg_y[t][:, 0:LAYS], y_rest[t - 1][:], ACT.Copy, scale=-1.0)
            pieces = ((0, 512), (512, 512)) if t < PACK - 1 else ((0, 512), (512, 256), (768, 256))
            for j0, width in pieces[1:] if t == 0 else pieces:
                square = held("square%d_%d" % (t, j0), [P, width], F32)
                nc.scalar.activation(square[:], hs[t][:, j0 : j0 + width], ACT.Square)
                finish(t, j0, width, square)
